import numpy as np, ml_dtypes
CORES = [51,54,179,182]
N = 4
VB, TK = 4, 128
def setup_inputs(rng):
    h = rng.standard_normal((128, TK), dtype=np.float32) / 4; w = rng.standard_normal((N, 128, VB * 128), dtype=np.float32)
    a = 2 * np.pi * rng.random((TK)); s = 400 * rng.random((TK)) ** 1.5; h[0] = s * np.cos(a); h[1] = s * np.sin(a); h[2] = 150 * rng.standard_normal((TK)); w[:, 2, :] = 1 + w[:, 2, :] / 50
    a = (2 * np.pi * rng.random() + np.pi / 2 * (rng.permutation(N).reshape(N, 1, 1) + 0.5) / N - 0.5 + (np.arange(VB).reshape(1, VB, 1) + rng.random((N, VB, 128))) / VB).reshape(N, VB * 128); w[:, 0, :] = np.cos(a); w[:, 1, :] = np.sin(a)
    tgt = rng.integers(0, N * VB * 128, size=TK)
    oh = np.zeros((N * VB * 128, TK), np.float32); oh[tgt, np.arange(TK)] = 1.0
    oh = oh.reshape(N, VB, 128, TK).transpose(0, 2, 1, 3).reshape(N, 128, VB * TK)
    return {"h": np.broadcast_to(h, (N, 128, TK)).astype(ml_dtypes.bfloat16), "w": w.astype(ml_dtypes.bfloat16), "oh": oh.astype(ml_dtypes.bfloat16)}
def reference(h, w, oh):
    H, W, OH = h.astype(np.float64), w.astype(np.float64), oh.astype(np.float64)
    Z = np.concatenate([W[r].T @ H[r] for r in range(N)], axis=0)
    O = np.concatenate([OH[r][:, TK * b:TK * b + TK] for r in range(N) for b in range(VB)], axis=0)
    m = Z.max(axis=0)
    l = m + np.log(np.exp(Z - m).sum(axis=0)) - (O * Z).sum(axis=0)
    return {"l": np.broadcast_to(l.astype(np.float32), (N, 1, TK))}

@@ -1,0 +1,182 @@
+import math
+from concourse.bass import DstId, RemoteDMATransfer
+from concourse.mybir import AluOpType, AxisListType, ActivationFunctionType
+
+NK = 64
+D1 = 6.3 / NK
+D2 = 1.40 / NK
+G0 = D2 / (math.exp(D2) - 1.0)
+KAPPA = (NK / 2 + 0.5) * D1 + 0.5
+ENG_OFF = 4
+ENG_ON = 4
+
+SCRATCH = {
+    "h_sb": ("sbuf", [128, 128], "bfloat16"),
+    "w_sb": ("sbuf", [128, 512], "bfloat16"),
+    "oh_sb": ("sbuf", [128, 512], "bfloat16"),
+    "ones_bf": ("sbuf", [128, 128], "bfloat16"),
+    "ident": ("sbuf", [128, 128], "bfloat16"),
+    "jt": ("sbuf", [128, NK], "float32"),
+    "r1": ("sbuf", [128, NK], "float32"),
+    "r2": ("sbuf", [128, NK], "float32"),
+    "wT_sb": ("sbuf", [128, 512], "bfloat16"),
+    "hT_sb": ("sbuf", [128, 128], "bfloat16"),
+    "junk": ("sbuf", [128, 512], "float32"),
+    "junk2": ("sbuf", [128, NK], "float32"),
+    "prod": ("sbuf", [128, 128], "float32"),
+    "st": ("sbuf", [128, 16], "float32"),
+    "land": ("sbuf", [128, 16], "float32"),
+    "tbuf": ("sbuf", [128, 32], "float32"),
+    "tout": ("sbuf", [128, 32], "float32"),
+    "z_ps": ("psum", [128, 512], "float32"),
+    "g_ps": ("psum", [128, 512], "float32"),
+    "hT_ps": ("psum", [128, 1024], "bfloat16"),
+    "wT_ps0": ("psum", [128, 1024], "bfloat16"),
+    "wT_ps1": ("psum", [128, 1024], "bfloat16"),
+    "wT_ps2": ("psum", [128, 1024], "bfloat16"),
+    "wT_ps3": ("psum", [128, 1024], "bfloat16"),
+}
+SEMAPHORES = ["ld_h", "ld_w", "ld_oh", "ones", "tz", "iota", "ident", "r1", "r2", "hTp", "hTs", "z", "negm",
+              "wTp0", "wTp1", "wTp2", "wTp3", "wTs0", "wTs1", "wTs2", "wTs3", "gp", "s", "kp", "q", "sq", "c1", "a",
+              "prod", "t", "sent", "arrived", "negA", "S", "acc", "Ts", "d", "c", "fin", "tr", "out"]
+
+
+def _bits(mask):
+    return [e for e in range(mask.bit_length()) if (mask >> e) & 1]
+
+
+def _plan(src, cores, topo):
+    others = [d for d in cores if d != src]
+    near = [d for d in others if topo.host(d) == topo.host(src) and topo.chip(d) == topo.chip(src)]
+    far = [d for d in others if d not in near]
+    far_eng = _bits(topo.mask(src, far[0])) if far else []
+    plan = {}
+    for k, d in enumerate(far):
+        plan[d] = sum(1 << e for e in far_eng[k * ENG_OFF:(k + 1) * ENG_OFF])
+    used = far_eng[:len(far) * ENG_OFF]
+    for d in near:
+        free = [e for e in _bits(topo.mask(src, d)) if e not in far_eng and e not in used]
+        plan[d] = sum(1 << e for e in free[:ENG_ON])
+        used = used + free[:ENG_ON]
+    return plan
+
+
+def rank_program(g, core, T, topo):
+    rank = T.rank_of(core)
+    if rank is None:
+        return
+    S = T.sem
+    v, act, pe, sy = g.vector, g.scalar, g.tensor, g.sync
+    AF, OP, X = ActivationFunctionType, AluOpType, AxisListType.X
+    st = T.st
+    col = lambda k: st[:, k:k + 1]
+    NEGM, SS, KP, Q, SQ, C1, NEGA, SB, ACC, TS, DD, CC = [col(k) for k in range(12)]
+    own = 4 * rank
+    a_all, t_all = T.land[:, 0:16:4], T.land[:, 1:16:4]
+    blk = lambda b: slice(128 * b, 128 * b + 128)
+    wT_ps = [T.wT_ps0, T.wT_ps1, T.wT_ps2, T.wT_ps3]
+    wTp = [S.wTp0, S.wTp1, S.wTp2, S.wTp3]
+    wTs = [S.wTs0, S.wTs1, S.wTs2, S.wTs3]
+
+    act.dma_start(T.h_sb[:, :], T.h[:, :]).then_inc(S.ld_h, 16)
+    sy.dma_start(T.w_sb[:, :], T.w[:, :]).then_inc(S.ld_w, 16)
+    sy.dma_start(T.oh_sb[:, :], T.oh[:, :]).then_inc(S.ld_oh, 16)
+
+    v.memset(T.ones_bf[:, :], 1.0).then_inc(S.ones, 1)
+    v.memset(T.tbuf[:, :], 0.0).then_inc(S.tz, 1)
+    g.iota(T.jt[:, :], [[1, NK]], 1, 0, allow_small_or_imprecise_dtypes=True).then_inc(S.iota, 1)
+    g.wait_ge(S.ones, 1)
+    g.affine_select(T.ident[:, :], T.ones_bf[:, :], [[-1, 128]], OP.is_equal, 0.0, 0, 1).then_inc(S.ident, 1)
+    act.wait_ge(S.iota, 1)
+    act.activation(T.r1[:, :], T.jt[:, :], AF.Exp, scale=-D1).then_inc(S.r1, 1)
+    act.activation(T.r2[:, :], T.jt[:, :], AF.Exp, scale=-D2).then_inc(S.r2, 1)
+
+    pe.wait_ge(S.ident, 1)
+    pe.wait_ge(S.ld_h, 16)
+    pe.transpose(T.hT_ps[:, 0:128], T.h_sb[:, :], T.ident[:, :]).then_inc(S.hTp, 1)
+    pe.wait_ge(S.ld_w, 16)
+    pe.matmul(T.z_ps[:, :], T.h_sb[:, :], T.w_sb[:, :], True, True).then_inc(S.z, 1)
+    for b in range(4):
+        pe.transpose(wT_ps[b][:, 0:128], T.w_sb[:, blk(b)], T.ident[:, :]).then_inc(wTp[b], 1)
+    pe.wait_ge(S.ld_oh, 16)
+    for b in range(4):
+        pe.wait_ge(wTs[b], 1)
+        mm = pe.matmul(T.g_ps[:, 0:128], T.oh_sb[:, blk(b)], T.wT_sb[:, blk(b)], b == 0, b == 3)
+    mm.then_inc(S.gp, 1)
+
+    v.wait_ge(S.hTp, 1)
+    v.tensor_copy(T.hT_sb[:, :], T.hT_ps[:, 0:128]).then_inc(S.hTs, 1)
+    v.wait_ge(S.z, 1)
+    v.tensor_reduce(NEGM, T.z_ps[:, :], X, OP.max, negate=True).then_inc(S.negm, 1)
+    v.wait_ge(wTp[3], 1)
+    v.tensor_copy(T.wT_sb[:, blk(3)], wT_ps[3][:, 0:128]).then_inc(wTs[3], 1)
+    v.wait_ge(S.kp, 1)
+    v.wait_ge(S.negm, 1)
+    v.tensor_scalar(C1, KP, D1 / 2, NEGM, OP.mult, OP.subtract).then_inc(S.c1, 1)
+    v.wait_ge(S.gp, 1)
+    v.wait_ge(S.hTs, 1)
+    v.tensor_tensor(T.prod[:, :], T.g_ps[:, 0:128], T.hT_sb[:, :], OP.mult).then_inc(S.prod, 1)
+    v.wait_ge(S.prod, 1)
+    v.tensor_reduce(T.land[:, own + 1:own + 2], T.prod[:, :], X, OP.add).then_inc(S.t, 1)
+
+    for b in range(3):
+        act.wait_ge(wTp[b], 1)
+        act.activation(T.wT_sb[:, blk(b)], wT_ps[b][:, 0:128], AF.Copy).then_inc(wTs[b], 1)
+    act.wait_ge(S.negm, 1)
+    act.activation(T.junk[:, :], T.z_ps[:, :], AF.Exp, bias=NEGM, accum_out=SS).then_inc(S.s, 1)
+    act.wait_ge(S.s, 1)
+    act.wait_ge(S.r1, 1)
+    act.activation(T.junk2[:, :], T.r1[:, :], AF.Sign, bias=-1.0, scale=SS, accum_out=KP).then_inc(S.kp, 1)
+    act.wait_ge(S.kp, 1)
+    act.activation(Q, KP, AF.Exp, bias=-(NK / 2 + 0.5) * D1, scale=-D1 / 2).then_inc(S.q, 1)
+    act.wait_ge(S.q, 1)
+    act.activation(SQ, Q, AF.Square, bias=-2.0, scale=SS).then_inc(S.sq, 1)
+    act.wait_ge(S.sq, 1)
+    act.wait_ge(S.c1, 1)
+    act.activation(T.land[:, own:own + 1], SQ, AF.Identity, bias=C1, scale=-0.5).then_inc(S.a, 1)
+
+    plan = _plan(core, T.cores, topo)
+    transfers = []
+    for d in T.cores:
+        if d == core:
+            continue
+        rid, pid = topo.addr(d, core)
+        transfers.append(RemoteDMATransfer(dst_ids=[DstId(rid=rid, pnc=pid)], dma_engine_mask=plan[d],
+                                           remote_sem=S.arrived, src=T.land[:, own:own + 2],
+                                           dst=T.land[:, own:own + 2]))
+    g.wait_ge(S.a, 1)
+    g.wait_ge(S.t, 1)
+    g.remote_dma_fused(transfers, local_sem=S.sent)
+    n_in = sum(len(_bits(_plan(s, T.cores, topo)[core])) for s in T.cores if s != core)
+    n_out = sum(len(_bits(m)) for m in plan.values())
+
+    v.wait_ge(S.arrived, n_in)
+    v.wait_ge(S.a, 1)
+    v.wait_ge(S.t, 1)
+    v.tensor_reduce(NEGA, a_all, X, OP.max, negate=True).then_inc(S.negA, 1)
+    v.tensor_reduce(TS, t_all, X, OP.add).then_inc(S.Ts, 1)
+    v.wait_ge(S.negA, 1)
+    v.wait_ge(S.Ts, 1)
+    v.tensor_scalar(DD, TS, NEGA, -(KAPPA - G0 + D2 * D2 / 16), OP.add, OP.add).then_inc(S.d, 1)
+    v.wait_ge(S.S, 1)
+    v.wait_ge(S.d, 1)
+    v.tensor_scalar(CC, SB, G0, DD, OP.mult, OP.subtract).then_inc(S.c, 1)
+    v.wait_ge(S.acc, 1)
+    v.wait_ge(S.c, 1)
+    v.wait_ge(S.tz, 1)
+    v.tensor_scalar(T.tbuf[:, 0:1], ACC, -D2, CC, OP.mult, OP.add).then_inc(S.fin, 1)
+    v.wait_ge(S.fin, 1)
+    v.transpose(T.tout[:, :], T.tbuf[:, :]).then_inc(S.tr, 1)
+
+    act.wait_ge(S.arrived, n_in)
+    act.wait_ge(S.a, 1)
+    act.wait_ge(S.negA, 1)
+    act.activation(T.junk2[:, 0:4], a_all, AF.Exp, bias=NEGA, accum_out=SB).then_inc(S.S, 1)
+    act.wait_ge(S.S, 1)
+    act.wait_ge(S.r2, 1)
+    act.activation(T.junk2[:, :], T.r2[:, :], AF.Relu, bias=-1.0, scale=SB, accum_out=ACC).then_inc(S.acc, 1)
+
+    sy.wait_ge(S.tr, 1)
+    sy.dma_start(T.l[:, :], T.tout[0:128:32, :]).then_inc(S.out, 16)
+    sy.wait_ge(S.out, 16)
+    g.wait_ge(S.sent, n_out)

@@ -2,11 +2,9 @@ import math
 from concourse.bass import DstId, RemoteDMATransfer
 from concourse.mybir import AluOpType, AxisListType, ActivationFunctionType
 
-NK = 64
-D1 = 6.3 / NK
-D2 = 1.40 / NK
-G0 = D2 / (math.exp(D2) - 1.0)
-KAPPA = (NK / 2 + 0.5) * D1 + 0.5
+NK = 128
+D1 = 7.7 / NK
+G0 = D1 / (math.exp(D1) - 1.0)
 ENG_OFF = 4
 ENG_ON = 4
 
@@ -18,27 +16,31 @@ SCRATCH = {
     "ident": ("sbuf", [128, 128], "bfloat16"),
     "jt": ("sbuf", [128, NK], "float32"),
     "r1": ("sbuf", [128, NK], "float32"),
-    "r2": ("sbuf", [128, NK], "float32"),
     "wT_sb": ("sbuf", [128, 512], "bfloat16"),
     "hT_sb": ("sbuf", [128, 128], "bfloat16"),
     "junk": ("sbuf", [128, 512], "float32"),
     "junk2": ("sbuf", [128, NK], "float32"),
     "prod": ("sbuf", [128, 128], "float32"),
+    "wgt": ("sbuf", [128, 16], "float32"),
+    "ws": ("sbuf", [128, 16], "float32"),
     "st": ("sbuf", [128, 16], "float32"),
-    "land": ("sbuf", [128, 16], "float32"),
+    "land1": ("sbuf", [128, 32], "float32"),
+    "land2": ("sbuf", [128, 28], "float32"),
     "tbuf": ("sbuf", [128, 32], "float32"),
     "tout": ("sbuf", [128, 32], "float32"),
-    "z_ps": ("psum", [128, 512], "float32"),
+    "z_ps0": ("psum", [128, 512], "float32"),
+    "z_ps1": ("psum", [128, 512], "float32"),
+    "z_ps2": ("psum", [128, 512], "float32"),
+    "z_ps3": ("psum", [128, 512], "float32"),
     "g_ps": ("psum", [128, 512], "float32"),
     "hT_ps": ("psum", [128, 1024], "bfloat16"),
     "wT_ps0": ("psum", [128, 1024], "bfloat16"),
     "wT_ps1": ("psum", [128, 1024], "bfloat16"),
-    "wT_ps2": ("psum", [128, 1024], "bfloat16"),
-    "wT_ps3": ("psum", [128, 1024], "bfloat16"),
 }
-SEMAPHORES = ["ld_h", "ld_w", "ld_oh", "ones", "tz", "iota", "ident", "r1", "r2", "hTp", "hTs", "z", "negm",
-              "wTp0", "wTp1", "wTp2", "wTp3", "wTs0", "wTs1", "wTs2", "wTs3", "gp", "s", "kp", "q", "sq", "c1", "a",
-              "prod", "t", "sent", "arrived", "negA", "S", "acc", "Ts", "d", "c", "fin", "tr", "out"]
+SEMAPHORES = ["ld_h", "ld_w", "ld_oh", "ones", "tz", "cst", "iota", "ident", "r1", "hTp", "hTs",
+              "z0", "z1", "z2", "z3", "nm0", "nm1", "nm2", "nm3", "s0", "s1", "s2", "s3",
+              "wTp0", "wTp1", "wTp2", "wTp3", "wTs0", "wTs1", "wTs2", "wTs3", "gp", "prod", "t",
+              "sent", "arr1", "arr2", "negM", "wgt", "ws", "S", "acc", "b", "fin", "tr", "out"]
 
 
 def _bits(mask):
@@ -68,13 +70,15 @@ def rank_program(g, core, T, topo):
     S = T.sem
     v, act, pe, sy = g.vector, g.scalar, g.tensor, g.sync
     AF, OP, X = ActivationFunctionType, AluOpType, AxisListType.X
-    st = T.st
-    col = lambda k: st[:, k:k + 1]
-    NEGM, SS, KP, Q, SQ, C1, NEGA, SB, ACC, TS, DD, CC = [col(k) for k in range(12)]
-    own = 4 * rank
-    a_all, t_all = T.land[:, 0:16:4], T.land[:, 1:16:4]
+    NEGM, SB = T.st[:, 0:1], T.st[:, 1:2]
+    o1, o2 = 8 * rank, 4 * rank
+    nm_all, s_all = T.land1[:, 0:32:2], T.land1[:, 1:32:2]
     blk = lambda b: slice(128 * b, 128 * b + 128)
-    wT_ps = [T.wT_ps0, T.wT_ps1, T.wT_ps2, T.wT_ps3]
+    z_ps = [T.z_ps0, T.z_ps1, T.z_ps2, T.z_ps3]
+    wT_ps = [T.wT_ps0, T.wT_ps1, T.wT_ps0, T.wT_ps1]
+    zs = [S.z0, S.z1, S.z2, S.z3]
+    nms = [S.nm0, S.nm1, S.nm2, S.nm3]
+    ssm = [S.s0, S.s1, S.s2, S.s3]
     wTp = [S.wTp0, S.wTp1, S.wTp2, S.wTp3]
     wTs = [S.wTs0, S.wTs1, S.wTs2, S.wTs3]
 
@@ -84,99 +88,95 @@ def rank_program(g, core, T, topo):
 
     v.memset(T.ones_bf[:, :], 1.0).then_inc(S.ones, 1)
     v.memset(T.tbuf[:, :], 0.0).then_inc(S.tz, 1)
+    v.memset(T.land2[:, 24:28], G0 - D1 * D1 / 16).then_inc(S.cst, 1)
     g.iota(T.jt[:, :], [[1, NK]], 1, 0, allow_small_or_imprecise_dtypes=True).then_inc(S.iota, 1)
     g.wait_ge(S.ones, 1)
     g.affine_select(T.ident[:, :], T.ones_bf[:, :], [[-1, 128]], OP.is_equal, 0.0, 0, 1).then_inc(S.ident, 1)
     act.wait_ge(S.iota, 1)
-    act.activation(T.r1[:, :], T.jt[:, :], AF.Exp, scale=-D1).then_inc(S.r1, 1)
-    act.activation(T.r2[:, :], T.jt[:, :], AF.Exp, scale=-D2).then_inc(S.r2, 1)
+    act.activation(T.r1[:, :], T.jt[:, :], AF.Exp, bias=math.log(D1), scale=-D1).then_inc(S.r1, 1)
 
-    pe.wait_ge(S.ident, 1)
     pe.wait_ge(S.ld_h, 16)
-    pe.transpose(T.hT_ps[:, 0:128], T.h_sb[:, :], T.ident[:, :]).then_inc(S.hTp, 1)
     pe.wait_ge(S.ld_w, 16)
-    pe.matmul(T.z_ps[:, :], T.h_sb[:, :], T.w_sb[:, :], True, True).then_inc(S.z, 1)
+    for c in range(4):
+        pe.matmul(z_ps[c][:, 0:128], T.h_sb[:, :], T.w_sb[:, blk(c)], True, True).then_inc(zs[c], 1)
+    pe.wait_ge(S.ident, 1)
     for b in range(4):
+        if b >= 2:
+            pe.wait_ge(wTs[b - 2], 1)
         pe.transpose(wT_ps[b][:, 0:128], T.w_sb[:, blk(b)], T.ident[:, :]).then_inc(wTp[b], 1)
+    pe.transpose(T.hT_ps[:, 0:128], T.h_sb[:, :], T.ident[:, :]).then_inc(S.hTp, 1)
     pe.wait_ge(S.ld_oh, 16)
     for b in range(4):
         pe.wait_ge(wTs[b], 1)
         mm = pe.matmul(T.g_ps[:, 0:128], T.oh_sb[:, blk(b)], T.wT_sb[:, blk(b)], b == 0, b == 3)
     mm.then_inc(S.gp, 1)
 
+    for c in range(4):
+        v.wait_ge(zs[c], 1)
+        v.tensor_reduce(T.land1[:, o1 + 2 * c:o1 + 2 * c + 1], z_ps[c][:, 0:128], X, OP.max, negate=True).then_inc(nms[c], 1)
+    for b in range(4):
+        v.wait_ge(wTp[b], 1)
+        v.tensor_copy(T.wT_sb[:, blk(b)], wT_ps[b][:, 0:128]).then_inc(wTs[b], 1)
     v.wait_ge(S.hTp, 1)
     v.tensor_copy(T.hT_sb[:, :], T.hT_ps[:, 0:128]).then_inc(S.hTs, 1)
-    v.wait_ge(S.z, 1)
-    v.tensor_reduce(NEGM, T.z_ps[:, :], X, OP.max, negate=True).then_inc(S.negm, 1)
-    v.wait_ge(wTp[3], 1)
-    v.tensor_copy(T.wT_sb[:, blk(3)], wT_ps[3][:, 0:128]).then_inc(wTs[3], 1)
-    v.wait_ge(S.kp, 1)
-    v.wait_ge(S.negm, 1)
-    v.tensor_scalar(C1, KP, D1 / 2, NEGM, OP.mult, OP.subtract).then_inc(S.c1, 1)
     v.wait_ge(S.gp, 1)
     v.wait_ge(S.hTs, 1)
     v.tensor_tensor(T.prod[:, :], T.g_ps[:, 0:128], T.hT_sb[:, :], OP.mult).then_inc(S.prod, 1)
     v.wait_ge(S.prod, 1)
-    v.tensor_reduce(T.land[:, own + 1:own + 2], T.prod[:, :], X, OP.add).then_inc(S.t, 1)
+    v.tensor_reduce(T.land2[:, o2:o2 + 1], T.prod[:, :], X, OP.add).then_inc(S.t, 1)
 
-    for b in range(3):
-        act.wait_ge(wTp[b], 1)
-        act.activation(T.wT_sb[:, blk(b)], wT_ps[b][:, 0:128], AF.Copy).then_inc(wTs[b], 1)
-    act.wait_ge(S.negm, 1)
-    act.activation(T.junk[:, :], T.z_ps[:, :], AF.Exp, bias=NEGM, accum_out=SS).then_inc(S.s, 1)
-    act.wait_ge(S.s, 1)
-    act.wait_ge(S.r1, 1)
-    act.activation(T.junk2[:, :], T.r1[:, :], AF.Sign, bias=-1.0, scale=SS, accum_out=KP).then_inc(S.kp, 1)
-    act.wait_ge(S.kp, 1)
-    act.activation(Q, KP, AF.Exp, bias=-(NK / 2 + 0.5) * D1, scale=-D1 / 2).then_inc(S.q, 1)
-    act.wait_ge(S.q, 1)
-    act.activation(SQ, Q, AF.Square, bias=-2.0, scale=SS).then_inc(S.sq, 1)
-    act.wait_ge(S.sq, 1)
-    act.wait_ge(S.c1, 1)
-    act.activation(T.land[:, own:own + 1], SQ, AF.Identity, bias=C1, scale=-0.5).then_inc(S.a, 1)
+    for c in range(4):
+        act.wait_ge(nms[c], 1)
+        act.activation(T.junk[:, blk(c)], z_ps[c][:, 0:128], AF.Exp, bias=T.land1[:, o1 + 2 * c:o1 + 2 * c + 1],
+                       accum_out=T.land1[:, o1 + 2 * c + 1:o1 + 2 * c + 2]).then_inc(ssm[c], 1)
 
     plan = _plan(core, T.cores, topo)
-    transfers = []
-    for d in T.cores:
-        if d == core:
-            continue
-        rid, pid = topo.addr(d, core)
-        transfers.append(RemoteDMATransfer(dst_ids=[DstId(rid=rid, pnc=pid)], dma_engine_mask=plan[d],
-                                           remote_sem=S.arrived, src=T.land[:, own:own + 2],
-                                           dst=T.land[:, own:own + 2]))
-    g.wait_ge(S.a, 1)
+
+    def send(ap, sem):
+        transfers = []
+        for d in T.cores:
+            if d != core:
+                rid, pid = topo.addr(d, core)
+                transfers.append(RemoteDMATransfer(dst_ids=[DstId(rid=rid, pnc=pid)], dma_engine_mask=plan[d],
+                                                   remote_sem=sem, src=ap, dst=ap))
+        g.remote_dma_fused(transfers, local_sem=S.sent)
+
+    for c in range(4):
+        g.wait_ge(ssm[c], 1)
+    send(T.land1[:, o1:o1 + 8], S.arr1)
     g.wait_ge(S.t, 1)
-    g.remote_dma_fused(transfers, local_sem=S.sent)
+    send(T.land2[:, o2:o2 + 1], S.arr2)
     n_in = sum(len(_bits(_plan(s, T.cores, topo)[core])) for s in T.cores if s != core)
     n_out = sum(len(_bits(m)) for m in plan.values())
 
-    v.wait_ge(S.arrived, n_in)
-    v.wait_ge(S.a, 1)
-    v.wait_ge(S.t, 1)
-    v.tensor_reduce(NEGA, a_all, X, OP.max, negate=True).then_inc(S.negA, 1)
-    v.tensor_reduce(TS, t_all, X, OP.add).then_inc(S.Ts, 1)
-    v.wait_ge(S.negA, 1)
-    v.wait_ge(S.Ts, 1)
-    v.tensor_scalar(DD, TS, NEGA, -(KAPPA - G0 + D2 * D2 / 16), OP.add, OP.add).then_inc(S.d, 1)
+    v.wait_ge(S.arr1, n_in)
+    for c in range(4):
+        v.wait_ge(ssm[c], 1)
+    v.tensor_reduce(NEGM, nm_all, X, OP.min).then_inc(S.negM, 1)
+    act.wait_ge(S.arr1, n_in)
+    act.wait_ge(S.negM, 1)
+    act.activation(T.wgt[:, :], nm_all, AF.Exp, bias=NEGM, scale=-1.0).then_inc(S.wgt, 1)
+    v.wait_ge(S.wgt, 1)
+    v.tensor_tensor(T.ws[:, :], s_all, T.wgt[:, :], OP.mult).then_inc(S.ws, 1)
+    v.wait_ge(S.ws, 1)
+    v.tensor_reduce(SB, T.ws[:, :], X, OP.add).then_inc(S.S, 1)
+    act.wait_ge(S.S, 1)
+    act.wait_ge(S.r1, 1)
+    act.activation(T.junk2[:, :], T.r1[:, :], AF.Relu, bias=-D1, scale=SB, accum_out=T.land2[:, 20:21]).then_inc(S.acc, 1)
     v.wait_ge(S.S, 1)
-    v.wait_ge(S.d, 1)
-    v.tensor_scalar(CC, SB, G0, DD, OP.mult, OP.subtract).then_inc(S.c, 1)
+    v.wait_ge(S.negM, 1)
+    v.tensor_scalar(T.land2[:, 16:17], SB, -G0, NEGM, OP.mult, OP.add).then_inc(S.b, 1)
+
+    v.wait_ge(S.arr2, n_in)
     v.wait_ge(S.acc, 1)
-    v.wait_ge(S.c, 1)
+    v.wait_ge(S.b, 1)
+    v.wait_ge(S.t, 1)
+    v.wait_ge(S.cst, 1)
     v.wait_ge(S.tz, 1)
-    v.tensor_scalar(T.tbuf[:, 0:1], ACC, -D2, CC, OP.mult, OP.add).then_inc(S.fin, 1)
+    v.tensor_reduce(T.tbuf[:, 0:1], T.land2[:, 0:28:4], X, OP.add, negate=True).then_inc(S.fin, 1)
     v.wait_ge(S.fin, 1)
     v.transpose(T.tout[:, :], T.tbuf[:, :]).then_inc(S.tr, 1)
-
-    act.wait_ge(S.arrived, n_in)
-    act.wait_ge(S.a, 1)
-    act.wait_ge(S.negA, 1)
-    act.activation(T.junk2[:, 0:4], a_all, AF.Exp, bias=NEGA, accum_out=SB).then_inc(S.S, 1)
-    act.wait_ge(S.S, 1)
-    act.wait_ge(S.r2, 1)
-    act.activation(T.junk2[:, :], T.r2[:, :], AF.Relu, bias=-1.0, scale=SB, accum_out=ACC).then_inc(S.acc, 1)
-
     sy.wait_ge(S.tr, 1)
     sy.dma_start(T.l[:, :], T.tout[0:128:32, :]).then_inc(S.out, 16)
     sy.wait_ge(S.out, 16)
-    g.wait_ge(S.sent, n_out)
+    g.wait_ge(S.sent, 2 * n_out)

@@ -3,6 +3,7 @@ from concourse.bass import DstId, RemoteDMATransfer
 from concourse.mybir import AluOpType, AxisListType, ActivationFunctionType
 
 NK = 128
+NK0 = 8
 D1 = 7.7 / NK
 G0 = D1 / (math.exp(D1) - 1.0)
 ENG_OFF = 4
@@ -24,7 +25,8 @@ SCRATCH = {
     "wgt": ("sbuf", [128, 16], "float32"),
     "ws": ("sbuf", [128, 16], "float32"),
     "st": ("sbuf", [128, 16], "float32"),
-    "land1": ("sbuf", [128, 32], "float32"),
+    "landm": ("sbuf", [128, 16], "float32"),
+    "lands": ("sbuf", [128, 16], "float32"),
     "land2": ("sbuf", [128, 28], "float32"),
     "tbuf": ("sbuf", [128, 32], "float32"),
     "tout": ("sbuf", [128, 32], "float32"),
@@ -32,15 +34,15 @@ SCRATCH = {
     "z_ps1": ("psum", [128, 512], "float32"),
     "z_ps2": ("psum", [128, 512], "float32"),
     "z_ps3": ("psum", [128, 512], "float32"),
-    "g_ps": ("psum", [128, 512], "float32"),
-    "hT_ps": ("psum", [128, 1024], "bfloat16"),
     "wT_ps0": ("psum", [128, 1024], "bfloat16"),
     "wT_ps1": ("psum", [128, 1024], "bfloat16"),
+    "wT_ps2": ("psum", [128, 1024], "bfloat16"),
+    "wT_ps3": ("psum", [128, 1024], "bfloat16"),
 }
-SEMAPHORES = ["ld_h", "ld_w", "ld_oh", "ones", "tz", "cst", "iota", "ident", "r1", "hTp", "hTs",
+SEMAPHORES = ["ld_h", "ld_w", "ld_oh", "ones", "tz", "cst", "iota", "iotb", "ident", "r1", "r1b", "hTp", "hTs",
               "z0", "z1", "z2", "z3", "nm0", "nm1", "nm2", "nm3", "s0", "s1", "s2", "s3",
               "wTp0", "wTp1", "wTp2", "wTp3", "wTs0", "wTs1", "wTs2", "wTs3", "gp", "prod", "t",
-              "sent", "arr1", "arr2", "negM", "wgt", "ws", "S", "acc", "b", "fin", "tr", "out"]
+              "sent", "arrm", "arrs", "arr2", "negM", "wgt", "ws", "S", "acc", "b", "fin", "tr", "out"]
 
 
 def _bits(mask):
@@ -71,11 +73,11 @@ def rank_program(g, core, T, topo):
     v, act, pe, sy = g.vector, g.scalar, g.tensor, g.sync
     AF, OP, X = ActivationFunctionType, AluOpType, AxisListType.X
     NEGM, SB = T.st[:, 0:1], T.st[:, 1:2]
-    o1, o2 = 8 * rank, 4 * rank
-    nm_all, s_all = T.land1[:, 0:32:2], T.land1[:, 1:32:2]
+    o = 4 * rank
     blk = lambda b: slice(128 * b, 128 * b + 128)
     z_ps = [T.z_ps0, T.z_ps1, T.z_ps2, T.z_ps3]
-    wT_ps = [T.wT_ps0, T.wT_ps1, T.wT_ps0, T.wT_ps1]
+    wT_ps = [T.wT_ps0, T.wT_ps1, T.wT_ps2, T.wT_ps3]
+    hT_ps, g_ps = T.wT_ps0[:, 128:256], T.z_ps0[:, 128:256]
     zs = [S.z0, S.z1, S.z2, S.z3]
     nms = [S.nm0, S.nm1, S.nm2, S.nm3]
     ssm = [S.s0, S.s1, S.s2, S.s3]
@@ -89,11 +91,14 @@ def rank_program(g, core, T, topo):
     v.memset(T.ones_bf[:, :], 1.0).then_inc(S.ones, 1)
     v.memset(T.tbuf[:, :], 0.0).then_inc(S.tz, 1)
     v.memset(T.land2[:, 24:28], G0 - D1 * D1 / 16).then_inc(S.cst, 1)
-    g.iota(T.jt[:, :], [[1, NK]], 1, 0, allow_small_or_imprecise_dtypes=True).then_inc(S.iota, 1)
+    g.iota(T.jt[:, 0:NK0], [[1, NK0]], 1, 0, allow_small_or_imprecise_dtypes=True).then_inc(S.iota, 1)
+    g.iota(T.jt[:, NK0:NK], [[1, NK - NK0]], 1 + NK0, 0, allow_small_or_imprecise_dtypes=True).then_inc(S.iotb, 1)
     g.wait_ge(S.ones, 1)
     g.affine_select(T.ident[:, :], T.ones_bf[:, :], [[-1, 128]], OP.is_equal, 0.0, 0, 1).then_inc(S.ident, 1)
     act.wait_ge(S.iota, 1)
-    act.activation(T.r1[:, :], T.jt[:, :], AF.Exp, bias=math.log(D1), scale=-D1).then_inc(S.r1, 1)
+    act.activation(T.r1[:, 0:NK0], T.jt[:, 0:NK0], AF.Exp, bias=math.log(D1), scale=-D1).then_inc(S.r1, 1)
+    act.wait_ge(S.iotb, 1)
+    act.activation(T.r1[:, NK0:NK], T.jt[:, NK0:NK], AF.Exp, bias=math.log(D1), scale=-D1).then_inc(S.r1b, 1)
 
     pe.wait_ge(S.ld_h, 16)
     pe.wait_ge(S.ld_w, 16)
@@ -101,34 +106,34 @@ def rank_program(g, core, T, topo):
         pe.matmul(z_ps[c][:, 0:128], T.h_sb[:, :], T.w_sb[:, blk(c)], True, True).then_inc(zs[c], 1)
     pe.wait_ge(S.ident, 1)
     for b in range(4):
-        if b >= 2:
-            pe.wait_ge(wTs[b - 2], 1)
         pe.transpose(wT_ps[b][:, 0:128], T.w_sb[:, blk(b)], T.ident[:, :]).then_inc(wTp[b], 1)
-    pe.transpose(T.hT_ps[:, 0:128], T.h_sb[:, :], T.ident[:, :]).then_inc(S.hTp, 1)
+    pe.wait_ge(wTs[0], 1)
+    pe.transpose(hT_ps, T.h_sb[:, :], T.ident[:, :]).then_inc(S.hTp, 1)
+    pe.wait_ge(ssm[0], 1)
     pe.wait_ge(S.ld_oh, 16)
     for b in range(4):
         pe.wait_ge(wTs[b], 1)
-        mm = pe.matmul(T.g_ps[:, 0:128], T.oh_sb[:, blk(b)], T.wT_sb[:, blk(b)], b == 0, b == 3)
+        mm = pe.matmul(g_ps, T.oh_sb[:, blk(b)], T.wT_sb[:, blk(b)], b == 0, b == 3)
     mm.then_inc(S.gp, 1)
 
     for c in range(4):
         v.wait_ge(zs[c], 1)
-        v.tensor_reduce(T.land1[:, o1 + 2 * c:o1 + 2 * c + 1], z_ps[c][:, 0:128], X, OP.max, negate=True).then_inc(nms[c], 1)
+        v.tensor_reduce(T.landm[:, o + c:o + c + 1], z_ps[c][:, 0:128], X, OP.max, negate=True).then_inc(nms[c], 1)
     for b in range(4):
         v.wait_ge(wTp[b], 1)
         v.tensor_copy(T.wT_sb[:, blk(b)], wT_ps[b][:, 0:128]).then_inc(wTs[b], 1)
     v.wait_ge(S.hTp, 1)
-    v.tensor_copy(T.hT_sb[:, :], T.hT_ps[:, 0:128]).then_inc(S.hTs, 1)
+    v.tensor_copy(T.hT_sb[:, :], hT_ps).then_inc(S.hTs, 1)
     v.wait_ge(S.gp, 1)
     v.wait_ge(S.hTs, 1)
-    v.tensor_tensor(T.prod[:, :], T.g_ps[:, 0:128], T.hT_sb[:, :], OP.mult).then_inc(S.prod, 1)
+    v.tensor_tensor(T.prod[:, :], g_ps, T.hT_sb[:, :], OP.mult).then_inc(S.prod, 1)
     v.wait_ge(S.prod, 1)
-    v.tensor_reduce(T.land2[:, o2:o2 + 1], T.prod[:, :], X, OP.add).then_inc(S.t, 1)
+    v.tensor_reduce(T.land2[:, o:o + 1], T.prod[:, :], X, OP.add).then_inc(S.t, 1)
 
     for c in range(4):
         act.wait_ge(nms[c], 1)
-        act.activation(T.junk[:, blk(c)], z_ps[c][:, 0:128], AF.Exp, bias=T.land1[:, o1 + 2 * c:o1 + 2 * c + 1],
-                       accum_out=T.land1[:, o1 + 2 * c + 1:o1 + 2 * c + 2]).then_inc(ssm[c], 1)
+        act.activation(T.junk[:, blk(c)], z_ps[c][:, 0:128], AF.Exp, bias=T.landm[:, o + c:o + c + 1],
+                       accum_out=T.lands[:, o + c:o + c + 1]).then_inc(ssm[c], 1)
 
     plan = _plan(core, T.cores, topo)
 
@@ -142,26 +147,33 @@ def rank_program(g, core, T, topo):
         g.remote_dma_fused(transfers, local_sem=S.sent)
 
     for c in range(4):
+        g.wait_ge(nms[c], 1)
+    send(T.landm[:, o:o + 4], S.arrm)
+    for c in range(4):
         g.wait_ge(ssm[c], 1)
-    send(T.land1[:, o1:o1 + 8], S.arr1)
+    send(T.lands[:, o:o + 4], S.arrs)
     g.wait_ge(S.t, 1)
-    send(T.land2[:, o2:o2 + 1], S.arr2)
+    send(T.land2[:, o:o + 1], S.arr2)
     n_in = sum(len(_bits(_plan(s, T.cores, topo)[core])) for s in T.cores if s != core)
     n_out = sum(len(_bits(m)) for m in plan.values())
 
-    v.wait_ge(S.arr1, n_in)
+    v.wait_ge(S.arrm, n_in)
+    for c in range(4):
+        v.wait_ge(nms[c], 1)
+    v.tensor_reduce(NEGM, T.landm[:, :], X, OP.min).then_inc(S.negM, 1)
+    act.wait_ge(S.arrm, n_in)
+    act.wait_ge(S.negM, 1)
+    act.activation(T.wgt[:, :], T.landm[:, :], AF.Exp, bias=NEGM, scale=-1.0).then_inc(S.wgt, 1)
+    v.wait_ge(S.arrs, n_in)
     for c in range(4):
         v.wait_ge(ssm[c], 1)
-    v.tensor_reduce(NEGM, nm_all, X, OP.min).then_inc(S.negM, 1)
-    act.wait_ge(S.arr1, n_in)
-    act.wait_ge(S.negM, 1)
-    act.activation(T.wgt[:, :], nm_all, AF.Exp, bias=NEGM, scale=-1.0).then_inc(S.wgt, 1)
     v.wait_ge(S.wgt, 1)
-    v.tensor_tensor(T.ws[:, :], s_all, T.wgt[:, :], OP.mult).then_inc(S.ws, 1)
+    v.tensor_tensor(T.ws[:, :], T.lands[:, :], T.wgt[:, :], OP.mult).then_inc(S.ws, 1)
     v.wait_ge(S.ws, 1)
     v.tensor_reduce(SB, T.ws[:, :], X, OP.add).then_inc(S.S, 1)
     act.wait_ge(S.S, 1)
     act.wait_ge(S.r1, 1)
+    act.wait_ge(S.r1b, 1)
     act.activation(T.junk2[:, :], T.r1[:, :], AF.Relu, bias=-D1, scale=SB, accum_out=T.land2[:, 20:21]).then_inc(S.acc, 1)
     v.wait_ge(S.S, 1)
     v.wait_ge(S.negM, 1)
@@ -179,4 +191,4 @@ def rank_program(g, core, T, topo):
     sy.wait_ge(S.tr, 1)
     sy.dma_start(T.l[:, :], T.tout[0:128:32, :]).then_inc(S.out, 16)
     sy.wait_ge(S.out, 16)
-    g.wait_ge(S.sent, 2 * n_out)
+    g.wait_ge(S.sent, 3 * n_out)

@@ -2,7 +2,7 @@ import math
 from concourse.bass import DstId, RemoteDMATransfer
 from concourse.mybir import AluOpType, AxisListType, ActivationFunctionType
 
-NK = 128
+NK = 64
 NK0 = 8
 D1 = 7.7 / NK
 G0 = D1 / (math.exp(D1) - 1.0)
@@ -28,8 +28,7 @@ SCRATCH = {
     "landm": ("sbuf", [128, 16], "float32"),
     "lands": ("sbuf", [128, 16], "float32"),
     "land2": ("sbuf", [128, 28], "float32"),
-    "tbuf": ("sbuf", [128, 32], "float32"),
-    "tout": ("sbuf", [128, 32], "float32"),
+    "res": ("sbuf", [128, 4], "float32"),
     "z_ps0": ("psum", [128, 512], "float32"),
     "z_ps1": ("psum", [128, 512], "float32"),
     "z_ps2": ("psum", [128, 512], "float32"),
@@ -39,10 +38,10 @@ SCRATCH = {
     "wT_ps2": ("psum", [128, 1024], "bfloat16"),
     "wT_ps3": ("psum", [128, 1024], "bfloat16"),
 }
-SEMAPHORES = ["ld_h", "ld_w", "ld_oh", "ones", "tz", "cst", "iota", "iotb", "ident", "r1", "r1b", "hTp", "hTs",
+SEMAPHORES = ["ld_h", "ld_wa", "ld_wb", "ld_oh", "ones", "cst", "iota", "iotb", "ident", "r1", "r1b", "hTp", "hTs",
               "z0", "z1", "z2", "z3", "nm0", "nm1", "nm2", "nm3", "s0", "s1", "s2", "s3",
               "wTp0", "wTp1", "wTp2", "wTp3", "wTs0", "wTs1", "wTs2", "wTs3", "gp", "prod", "t",
-              "sent", "arrm", "arrs", "arr2", "negM", "wgt", "ws", "S", "acc", "b", "fin", "tr", "out"]
+              "sent", "arrm", "arrs", "arr2", "negM", "wgt", "ws", "S", "acc", "b", "fin", "out"]
 
 
 def _bits(mask):
@@ -85,11 +84,11 @@ def rank_program(g, core, T, topo):
     wTs = [S.wTs0, S.wTs1, S.wTs2, S.wTs3]
 
     act.dma_start(T.h_sb[:, :], T.h[:, :]).then_inc(S.ld_h, 16)
-    sy.dma_start(T.w_sb[:, :], T.w[:, :]).then_inc(S.ld_w, 16)
+    sy.dma_start(T.w_sb[:, 0:256], T.w[:, 0:256]).then_inc(S.ld_wa, 16)
+    sy.dma_start(T.w_sb[:, 256:512], T.w[:, 256:512]).then_inc(S.ld_wb, 16)
     sy.dma_start(T.oh_sb[:, :], T.oh[:, :]).then_inc(S.ld_oh, 16)
 
     v.memset(T.ones_bf[:, :], 1.0).then_inc(S.ones, 1)
-    v.memset(T.tbuf[:, :], 0.0).then_inc(S.tz, 1)
     v.memset(T.land2[:, 24:28], G0 - D1 * D1 / 16).then_inc(S.cst, 1)
     g.iota(T.jt[:, 0:NK0], [[1, NK0]], 1, 0, allow_small_or_imprecise_dtypes=True).then_inc(S.iota, 1)
     g.iota(T.jt[:, NK0:NK], [[1, NK - NK0]], 1 + NK0, 0, allow_small_or_imprecise_dtypes=True).then_inc(S.iotb, 1)
@@ -101,8 +100,10 @@ def rank_program(g, core, T, topo):
     act.activation(T.r1[:, NK0:NK], T.jt[:, NK0:NK], AF.Exp, bias=math.log(D1), scale=-D1).then_inc(S.r1b, 1)
 
     pe.wait_ge(S.ld_h, 16)
-    pe.wait_ge(S.ld_w, 16)
+    pe.wait_ge(S.ld_wa, 16)
     for c in range(4):
+        if c == 2:
+            pe.wait_ge(S.ld_wb, 16)
         pe.matmul(z_ps[c][:, 0:128], T.h_sb[:, :], T.w_sb[:, blk(c)], True, True).then_inc(zs[c], 1)
     pe.wait_ge(S.ident, 1)
     for b in range(4):
@@ -184,11 +185,8 @@ def rank_program(g, core, T, topo):
     v.wait_ge(S.b, 1)
     v.wait_ge(S.t, 1)
     v.wait_ge(S.cst, 1)
-    v.wait_ge(S.tz, 1)
-    v.tensor_reduce(T.tbuf[:, 0:1], T.land2[:, 0:28:4], X, OP.add, negate=True).then_inc(S.fin, 1)
-    v.wait_ge(S.fin, 1)
-    v.transpose(T.tout[:, :], T.tbuf[:, :]).then_inc(S.tr, 1)
-    sy.wait_ge(S.tr, 1)
-    sy.dma_start(T.l[:, :], T.tout[0:128:32, :]).then_inc(S.out, 16)
+    v.tensor_reduce(T.res[:, 0:1], T.land2[:, 0:28:4], X, OP.add, negate=True).then_inc(S.fin, 1)
+    sy.wait_ge(S.fin, 1)
+    sy.dma_start(T.l[:, :], T.res[:, 0:1]).then_inc(S.out, 16)
     sy.wait_ge(S.out, 16)
     g.wait_ge(S.sent, 3 * n_out)

import math
from concourse.bass import DstId, RemoteDMATransfer
from concourse.mybir import AluOpType, AxisListType, ActivationFunctionType

NK = 64
NK0 = 8
D1 = 7.7 / NK
G0 = D1 / (math.exp(D1) - 1.0)
ENG_OFF = 4
ENG_ON = 4

SCRATCH = {
    "h_sb": ("sbuf", [128, 128], "bfloat16"),
    "w_sb": ("sbuf", [128, 512], "bfloat16"),
    "oh_sb": ("sbuf", [128, 512], "bfloat16"),
    "ones_bf": ("sbuf", [128, 128], "bfloat16"),
    "ident": ("sbuf", [128, 128], "bfloat16"),
    "jt": ("sbuf", [128, NK], "float32"),
    "r1": ("sbuf", [128, NK], "float32"),
    "wT_sb": ("sbuf", [128, 512], "bfloat16"),
    "hT_sb": ("sbuf", [128, 128], "bfloat16"),
    "junk": ("sbuf", [128, 512], "float32"),
    "junk2": ("sbuf", [128, NK], "float32"),
    "prod": ("sbuf", [128, 128], "float32"),
    "wgt": ("sbuf", [128, 16], "float32"),
    "ws": ("sbuf", [128, 16], "float32"),
    "st": ("sbuf", [128, 16], "float32"),
    "landm": ("sbuf", [128, 16], "float32"),
    "lands": ("sbuf", [128, 16], "float32"),
    "land2": ("sbuf", [128, 28], "float32"),
    "res": ("sbuf", [128, 4], "float32"),
    "z_ps0": ("psum", [128, 512], "float32"),
    "z_ps1": ("psum", [128, 512], "float32"),
    "z_ps2": ("psum", [128, 512], "float32"),
    "z_ps3": ("psum", [128, 512], "float32"),
    "wT_ps0": ("psum", [128, 1024], "bfloat16"),
    "wT_ps1": ("psum", [128, 1024], "bfloat16"),
    "wT_ps2": ("psum", [128, 1024], "bfloat16"),
    "wT_ps3": ("psum", [128, 1024], "bfloat16"),
}
SEMAPHORES = ["ld_h", "ld_wa", "ld_wb", "ld_oh", "ones", "cst", "iota", "iotb", "ident", "r1", "r1b", "hTp", "hTs",
              "z0", "z1", "z2", "z3", "nm0", "nm1", "nm2", "nm3", "s0", "s1", "s2", "s3",
              "wTp0", "wTp1", "wTp2", "wTp3", "wTs0", "wTs1", "wTs2", "wTs3", "gp", "prod", "t",
              "sent", "arrm", "arrs", "arr2", "negM", "wgt", "ws", "S", "acc", "b", "fin", "out"]


def _bits(mask):
    return [e for e in range(mask.bit_length()) if (mask >> e) & 1]


def _plan(src, cores, topo):
    others = [d for d in cores if d != src]
    near = [d for d in others if topo.host(d) == topo.host(src) and topo.chip(d) == topo.chip(src)]
    far = [d for d in others if d not in near]
    far_eng = _bits(topo.mask(src, far[0])) if far else []
    plan = {}
    for k, d in enumerate(far):
        plan[d] = sum(1 << e for e in far_eng[k * ENG_OFF:(k + 1) * ENG_OFF])
    used = far_eng[:len(far) * ENG_OFF]
    for d in near:
        free = [e for e in _bits(topo.mask(src, d)) if e not in far_eng and e not in used]
        plan[d] = sum(1 << e for e in free[:ENG_ON])
        used = used + free[:ENG_ON]
    return plan


def rank_program(g, core, T, topo):
    rank = T.rank_of(core)
    if rank is None:
        return
    S = T.sem
    v, act, pe, sy = g.vector, g.scalar, g.tensor, g.sync
    AF, OP, X = ActivationFunctionType, AluOpType, AxisListType.X
    NEGM, SB = T.st[:, 0:1], T.st[:, 1:2]
    o = 4 * rank
    blk = lambda b: slice(128 * b, 128 * b + 128)
    z_ps = [T.z_ps0, T.z_ps1, T.z_ps2, T.z_ps3]
    wT_ps = [T.wT_ps0, T.wT_ps1, T.wT_ps2, T.wT_ps3]
    hT_ps, g_ps = T.wT_ps0[:, 128:256], T.z_ps0[:, 128:256]
    zs = [S.z0, S.z1, S.z2, S.z3]
    nms = [S.nm0, S.nm1, S.nm2, S.nm3]
    ssm = [S.s0, S.s1, S.s2, S.s3]
    wTp = [S.wTp0, S.wTp1, S.wTp2, S.wTp3]
    wTs = [S.wTs0, S.wTs1, S.wTs2, S.wTs3]

    act.dma_start(T.h_sb[:, :], T.h[:, :]).then_inc(S.ld_h, 16)
    sy.dma_start(T.w_sb[:, 0:256], T.w[:, 0:256]).then_inc(S.ld_wa, 16)
    sy.dma_start(T.w_sb[:, 256:512], T.w[:, 256:512]).then_inc(S.ld_wb, 16)
    sy.dma_start(T.oh_sb[:, :], T.oh[:, :]).then_inc(S.ld_oh, 16)

    v.memset(T.ones_bf[:, :], 1.0).then_inc(S.ones, 1)
    v.memset(T.land2[:, 24:28], G0 - D1 * D1 / 16).then_inc(S.cst, 1)
    g.iota(T.jt[:, 0:NK0], [[1, NK0]], 1, 0, allow_small_or_imprecise_dtypes=True).then_inc(S.iota, 1)
    g.iota(T.jt[:, NK0:NK], [[1, NK - NK0]], 1 + NK0, 0, allow_small_or_imprecise_dtypes=True).then_inc(S.iotb, 1)
    g.wait_ge(S.ones, 1)
    g.affine_select(T.ident[:, :], T.ones_bf[:, :], [[-1, 128]], OP.is_equal, 0.0, 0, 1).then_inc(S.ident, 1)
    act.wait_ge(S.iota, 1)
    act.activation(T.r1[:, 0:NK0], T.jt[:, 0:NK0], AF.Exp, bias=math.log(D1), scale=-D1).then_inc(S.r1, 1)
    act.wait_ge(S.iotb, 1)
    act.activation(T.r1[:, NK0:NK], T.jt[:, NK0:NK], AF.Exp, bias=math.log(D1), scale=-D1).then_inc(S.r1b, 1)

    pe.wait_ge(S.ld_h, 16)
    pe.wait_ge(S.ld_wa, 16)
    for c in range(4):
        if c == 2:
            pe.wait_ge(S.ld_wb, 16)
        pe.matmul(z_ps[c][:, 0:128], T.h_sb[:, :], T.w_sb[:, blk(c)], True, True).then_inc(zs[c], 1)
    pe.wait_ge(S.ident, 1)
    for b in range(4):
        pe.transpose(wT_ps[b][:, 0:128], T.w_sb[:, blk(b)], T.ident[:, :]).then_inc(wTp[b], 1)
    pe.wait_ge(wTs[0], 1)
    pe.transpose(hT_ps, T.h_sb[:, :], T.ident[:, :]).then_inc(S.hTp, 1)
    pe.wait_ge(ssm[0], 1)
    pe.wait_ge(S.ld_oh, 16)
    for b in range(4):
        pe.wait_ge(wTs[b], 1)
        mm = pe.matmul(g_ps, T.oh_sb[:, blk(b)], T.wT_sb[:, blk(b)], b == 0, b == 3)
    mm.then_inc(S.gp, 1)

    for c in range(4):
        v.wait_ge(zs[c], 1)
        v.tensor_reduce(T.landm[:, o + c:o + c + 1], z_ps[c][:, 0:128], X, OP.max, negate=True).then_inc(nms[c], 1)
    for b in range(4):
        v.wait_ge(wTp[b], 1)
        v.tensor_copy(T.wT_sb[:, blk(b)], wT_ps[b][:, 0:128]).then_inc(wTs[b], 1)
    v.wait_ge(S.hTp, 1)
    v.tensor_copy(T.hT_sb[:, :], hT_ps).then_inc(S.hTs, 1)
    v.wait_ge(S.gp, 1)
    v.wait_ge(S.hTs, 1)
    v.tensor_tensor(T.prod[:, :], g_ps, T.hT_sb[:, :], OP.mult).then_inc(S.prod, 1)
    v.wait_ge(S.prod, 1)
    v.tensor_reduce(T.land2[:, o:o + 1], T.prod[:, :], X, OP.add).then_inc(S.t, 1)

    for c in range(4):
        act.wait_ge(nms[c], 1)
        act.activation(T.junk[:, blk(c)], z_ps[c][:, 0:128], AF.Exp, bias=T.landm[:, o + c:o + c + 1],
                       accum_out=T.lands[:, o + c:o + c + 1]).then_inc(ssm[c], 1)

    plan = _plan(core, T.cores, topo)

    def send(ap, sem):
        transfers = []
        for d in T.cores:
            if d != core:
                rid, pid = topo.addr(d, core)
                transfers.append(RemoteDMATransfer(dst_ids=[DstId(rid=rid, pnc=pid)], dma_engine_mask=plan[d],
                                                   remote_sem=sem, src=ap, dst=ap))
        g.remote_dma_fused(transfers, local_sem=S.sent)

    for c in range(4):
        g.wait_ge(nms[c], 1)
    send(T.landm[:, o:o + 4], S.arrm)
    for c in range(4):
        g.wait_ge(ssm[c], 1)
    send(T.lands[:, o:o + 4], S.arrs)
    g.wait_ge(S.t, 1)
    send(T.land2[:, o:o + 1], S.arr2)
    n_in = sum(len(_bits(_plan(s, T.cores, topo)[core])) for s in T.cores if s != core)
    n_out = sum(len(_bits(m)) for m in plan.values())

    v.wait_ge(S.arrm, n_in)
    for c in range(4):
        v.wait_ge(nms[c], 1)
    v.tensor_reduce(NEGM, T.landm[:, :], X, OP.min).then_inc(S.negM, 1)
    act.wait_ge(S.arrm, n_in)
    act.wait_ge(S.negM, 1)
    act.activation(T.wgt[:, :], T.landm[:, :], AF.Exp, bias=NEGM, scale=-1.0).then_inc(S.wgt, 1)
    v.wait_ge(S.arrs, n_in)
    for c in range(4):
        v.wait_ge(ssm[c], 1)
    v.wait_ge(S.wgt, 1)
    v.tensor_tensor(T.ws[:, :], T.lands[:, :], T.wgt[:, :], OP.mult).then_inc(S.ws, 1)
    v.wait_ge(S.ws, 1)
    v.tensor_reduce(SB, T.ws[:, :], X, OP.add).then_inc(S.S, 1)
    act.wait_ge(S.S, 1)
    act.wait_ge(S.r1, 1)
    act.wait_ge(S.r1b, 1)
    act.activation(T.junk2[:, :], T.r1[:, :], AF.Relu, bias=-D1, scale=SB, accum_out=T.land2[:, 20:21]).then_inc(S.acc, 1)
    v.wait_ge(S.S, 1)
    v.wait_ge(S.negM, 1)
    v.tensor_scalar(T.land2[:, 16:17], SB, -G0, NEGM, OP.mult, OP.add).then_inc(S.b, 1)

    v.wait_ge(S.arr2, n_in)
    v.wait_ge(S.acc, 1)
    v.wait_ge(S.b, 1)
    v.wait_ge(S.t, 1)
    v.wait_ge(S.cst, 1)
    v.tensor_reduce(T.res[:, 0:1], T.land2[:, 0:28:4], X, OP.add, negate=True).then_inc(S.fin, 1)
    sy.wait_ge(S.fin, 1)
    sy.dma_start(T.l[:, :], T.res[:, 0:1]).then_inc(S.out, 16)
    sy.wait_ge(S.out, 16)
    g.wait_ge(S.sent, 3 * n_out)
